import numpy as np
import ml_dtypes


def mxq(x, axis, fmt="e4m3"):
    dtype, down = {"e4m3": (ml_dtypes.float8_e4m3fn, 7), "e5m2": (ml_dtypes.float8_e5m2, 14)}[fmt]
    v = np.moveaxis(np.asarray(x, np.float32).astype(ml_dtypes.bfloat16).astype(np.float64), axis, -1)
    blocks = v.reshape(v.shape[:-1] + (-1, 32))
    amax = np.abs(blocks).max(-1, keepdims=True)
    byte = np.maximum(np.where(amax > 0, np.frexp(amax)[1] - 1 + 127, 0) - down, 1)
    scale = np.exp2(byte - 127.0)
    codes = (blocks / scale).astype(np.float32).astype(dtype).astype(np.float64)
    return np.moveaxis((codes * scale).reshape(v.shape), -1, axis)


WIDE = False


def mx_kscale(k):
    if not WIDE:
        return np.ones(k)
    levels = np.array([10, -10, 5, -5, 0])
    if k % 512:
        return np.exp2(np.random.permutation(np.resize(levels, k // 32))).repeat(32)
    a = np.empty((k // 512, 16))
    for p in range(k // 512):
        a[p, :8] = np.random.permutation(np.resize(levels, 8))
        for g in range(8):
            far = levels[np.abs(levels - a[p, g]) >= 10]
            a[p, g + 8] = far[np.random.randint(len(far))]
    return np.exp2(a.ravel()).repeat(32)


BF16 = ml_dtypes.bfloat16


def bf(x):
    return np.asarray(x, np.float32).astype(BF16)


def f64(x):
    return np.asarray(x).astype(np.float64)


E2M1 = np.array([0.0, 0.5, 1.0, 1.5, 2.0, 3.0, 4.0, 6.0, -0.0, -0.5, -1.0, -1.5, -2.0, -3.0, -4.0, -6.0])


def pack_weight(w, fmt):
    k, n = w.shape
    w = f64(bf(w)).reshape(k // 32, 32, n)
    amax = np.abs(w).max(1)
    if fmt == "e4m3":
        byte = np.frexp(amax)[1] - 1 + 127 - 7
    else:
        mant, ex = np.frexp(amax / 6.0)
        byte = np.where(mant > 0.5, ex, ex - 1) + 127
    byte = np.clip(np.where(amax > 0, byte, 1), 1, 254)
    scaled = (w * np.exp2(127.0 - byte)[:, None, :]).reshape(k, n).astype(np.float32)
    by_word = np.ascontiguousarray(scaled.reshape(k // 512, 128, 4, n).transpose(0, 1, 3, 2))
    if fmt == "e4m3":
        words = by_word.astype(ml_dtypes.float8_e4m3fn).view(np.uint8)
    else:
        c = by_word.astype(ml_dtypes.float4_e2m1fn).view(np.uint8) & 0xF
        words = c[..., 0::2] | (c[..., 1::2] << 4)
    return np.ascontiguousarray(words), np.ascontiguousarray(byte.astype(np.uint8).reshape(k // 512, 16, n))


def unpack_weight(words, scales, fmt):
    g, p, n, _ = words.shape
    if fmt == "e4m3":
        vals = np.ascontiguousarray(words).view(ml_dtypes.float8_e4m3fn).astype(np.float64)
    else:
        nib = np.empty((g, p, n, 4), np.uint8)
        nib[..., 0::2] = words & 0xF
        nib[..., 1::2] = words >> 4
        vals = E2M1[nib]
    vals = vals * np.repeat(np.exp2(scales.astype(np.float64) - 127.0), 8, axis=1)[..., None]
    return vals.transpose(0, 1, 3, 2).reshape(g * 512, n)
def pack4(w):
    words, scales = pack_weight(w, "e2m1")
    return words.reshape(words.shape[0], 128, -1), scales


def unpack4(words, scales):
    return unpack_weight(words.reshape(words.shape[0], 128, -1, 2), scales, "e2m1")


def planes(Y):
    n, m = Y.shape
    b = f64(bf(Y)).reshape(n // 32, 32, m)
    amax = np.abs(b).max(1)
    byte = np.clip(np.where(amax > 0, np.frexp(amax)[1] - 1 + 127 - 7, 1), 1, 254)
    codes = (b * np.exp2(127.0 - byte)[:, None, :]).reshape(n, m).astype(np.float32).astype(ml_dtypes.float8_e4m3fn).view(np.uint8)
    words = codes.reshape(n // 512, 128, 4, m).transpose(0, 1, 3, 2)
    return np.ascontiguousarray(words), np.ascontiguousarray(byte.astype(np.uint8).reshape(n // 512, 16, m))


B, P, C, F = 4, 256, 1024, 2048
GELU_A, GELU_B = np.sqrt(2.0 / np.pi), 0.044715

def setup_inputs():
    s = mx_kscale(C)
    t = mx_kscale(F)
    x = np.random.randn(B, P, C) * s
    W1 = np.random.randn(C, F) / np.sqrt(C) / s[:, None]
    hid_scale = (1.0 + 0.1 * np.random.randn(F)) * t
    W2 = np.random.randn(F, C) / np.sqrt(F) / t[:, None]
    b2 = 0.3 * np.random.randn(C)
    out_scale = np.exp(0.8 * np.random.randn(C))
    skip = np.random.randn(B, P, C) * np.exp(0.8 * np.random.randn(C))
    w1_words, w1_scales = pack4(W1)
    w2_words, w2_scales = pack4(W2)
    return {"x": bf(x), "w1_words": w1_words, "w1_scales": w1_scales,
            "hid_scale": bf(hid_scale), "w2_words": w2_words, "w2_scales": w2_scales,
            "b2": bf(b2), "out_scale": bf(out_scale), "skip": bf(skip)}

def reference(x, w1_words, w1_scales, hid_scale, w2_words, w2_scales, b2, out_scale, skip):
    X = f64(x).reshape(B * P, C)
    W1 = unpack4(w1_words, w1_scales)
    W2 = unpack4(w2_words, w2_scales)
    Z = mxq(X, 1, "e4m3") @ W1
    H = 0.5 * Z * (1.0 + np.tanh(GELU_A * (Z + GELU_B * Z * Z * Z))) * f64(hid_scale)
    O = mxq(H, 1, "e4m3") @ W2
    y = f64(skip) + f64(out_scale) * (O + f64(b2)).reshape(B, P, C)
    Y = y.reshape(B * P, C).T
    words, scales = planes(Y)
    return y, words, scales

@@ -1,0 +1,409 @@
+from contextlib import ExitStack
+
+import concourse.mybir as mybir
+from concourse.masks import make_identity
+
+TOKENS, C, F = 1024, 1024, 2048
+FLOPS = 2 * 2 * TOKENS * C * F
+
+F32 = mybir.dt.float32
+BF16 = mybir.dt.bfloat16
+I32 = mybir.dt.int32
+U32 = mybir.dt.uint32
+U8 = mybir.dt.uint8
+FP8X4 = mybir.dt.float8_e4m3fn_x4
+FP4X4 = mybir.dt.float4_e2m1fn_x4
+ACT = mybir.ActivationFunctionType
+ALU = mybir.AluOpType
+
+P = 128
+BANK = 512
+K_PASS = 512
+TILES = TOKENS // P
+GC = C // K_PASS
+GF = F // K_PASS
+RING_BANKS = 6
+
+
+def tile_scaled_mixer_channel_mixing_h1_kernel(
+    tc, x, w1_words, w1_scales, hid_scale, w2_words, w2_scales, b2, out_scale, skip, out_0, out_1, out_2
+):
+    nc = tc.nc
+    x_rows = x.rearrange("b p c -> (b p) c")
+    skip_rows = skip.rearrange("b p c -> (b p) c")
+    y_rows = out_0.rearrange("b p c -> (b p) c")
+    words_out = out_1.rearrange("g p m t -> p g (m t)")
+
+    with ExitStack() as ctx:
+        keep = ctx.enter_context(tc.tile_pool(name="keep", bufs=1))
+        work = ctx.enter_context(tc.tile_pool(name="work", bufs=2))
+        deep = ctx.enter_context(tc.tile_pool(name="deep", bufs=3))
+        psum = ctx.enter_context(tc.psum_pool(name="psum", bufs=1))
+        ctx.enter_context(tc.manual_schedule())
+
+        taken = []
+
+        def next_bank():
+            tag = "bank%d" % (len(taken) % RING_BANKS)
+            bank = psum.tile([P, BANK], F32, name=tag, tag=tag)
+            taken.append(bank)
+            return bank
+
+        ident = keep.tile([P, P], F32, name="ident")
+        w1 = [keep.tile([P, GC, 2 * BANK], U8, name="w1_%d" % c, align_bytes=64) for c in range(GF)]
+        w2 = [keep.tile([P, GF, 2 * BANK], U8, name="w2_%d" % n, align_bytes=64) for n in range(GC)]
+        w1s = keep.tile([P, GC, F], U8, name="w1s", align_bytes=64)
+        w2s = keep.tile([P, GF, C], U8, name="w2s", align_bytes=64)
+        xs = [keep.tile([P, C], BF16, name="x_%d" % j, align_bytes=64) for j in range(TILES)]
+        skips = [keep.tile([P, C], BF16, name="skip_%d" % j, align_bytes=64) for j in range(TILES)]
+        hs_rows = keep.tile([P, GF, 4], BF16, name="hs_rows")
+        os_rows = keep.tile([P, C // P], BF16, name="os_rows")
+        b2_rows = keep.tile([P, C // P], BF16, name="b2_rows")
+        hs_banks = [psum.tile([P, BANK], F32, name="hs_bank%d" % h) for h in range(2)]
+        os_all = keep.tile([P, C], BF16, name="os_all", align_bytes=64)
+        b2_all = keep.tile([P, C], BF16, name="b2_all", align_bytes=64)
+        osb_all = keep.tile([P, C], F32, name="osb_all", align_bytes=64)
+        y_codes = keep.tile([P, GC, TOKENS], U32, name="y_codes", align_bytes=64)
+        y_scales = keep.tile([P, GC, TOKENS], U8, name="y_scales", align_bytes=64)
+        warm = keep.tile([P, 1], F32, name="warm")
+
+        def load_rows(dst, rows, j):
+            nc.sync.dma_start(out=dst[j][:], in_=rows[j * P : (j + 1) * P, :])
+
+        def load_words(dst, words, c):
+            src = words.rearrange("g p n -> p g n")[:, :, 2 * BANK * c : 2 * BANK * (c + 1)]
+            nc.sync.dma_start(out=dst[c][:].bitcast(I32), in_=src.bitcast(I32))
+
+        def load_scales(dst, scales):
+            for q in range(4):
+                src = scales[:, 4 * q : 4 * q + 4, :].rearrange("g r n -> r g n")
+                nc.sync.dma_start(out=dst[32 * q : 32 * q + 4, :, :].bitcast(I32), in_=src.bitcast(I32))
+
+        nc.vector.memset(w1s[:].bitcast(I32), 0)
+        nc.vector.memset(w2s[:].bitcast(I32), 0)
+        make_identity(nc, ident[:])
+        nc.scalar.dma_start(out=os_rows[:], in_=out_scale.rearrange("(p k) -> p k", p=P))
+        nc.scalar.dma_start(out=hs_rows[:], in_=hid_scale.rearrange("(g p k) -> p g k", g=GF, p=P))
+        nc.scalar.dma_start(out=b2_rows[:], in_=b2.rearrange("(p k) -> p k", p=P))
+        nc.scalar.activation(out=warm[:], in_=ident[:, 0:1], func=ACT.Gelu_apprx_tanh)
+
+        load_rows(xs, x_rows, 0)
+        load_scales(w1s, w1_scales)
+        load_words(w1, w1_words, 0)
+        load_words(w1, w1_words, 1)
+        load_rows(xs, x_rows, 1)
+        load_words(w1, w1_words, 2)
+        load_words(w1, w1_words, 3)
+        load_rows(xs, x_rows, 2)
+        load_scales(w2s, w2_scales)
+        load_words(w2, w2_words, 0)
+        load_rows(xs, x_rows, 3)
+        load_words(w2, w2_words, 1)
+        for j in range(TILES):
+            load_rows(skips, skip_rows, j)
+            if j + 4 < TILES:
+                load_rows(xs, x_rows, j + 4)
+
+        st = {}
+
+        def spread(bank, words):
+            for s in range(4):
+                nc.tensor.transpose(bank[:, s * P : (s + 1) * P], words[:, s : s + 1].to_broadcast([P, P]), ident[:])
+
+        def spread_channels(rows, dst):
+            bank = next_bank()
+            spread(bank, rows[:].bitcast(F32))
+            nc.scalar.copy(
+                out=dst[:].bitcast(F32).rearrange("p (n w) -> p n w", w=4),
+                in_=bank[:].rearrange("p (w n) -> p n w", w=4),
+            )
+
+        def spread_hidden(h):
+            words = hs_rows[:].rearrange("p g k -> p (g k)").bitcast(F32)
+            spread(hs_banks[h], words[:, 4 * h : 4 * h + 4])
+
+        def turn(key, sources):
+            bank = next_bank()
+            for s, src in enumerate(sources):
+                nc.tensor.transpose(bank[:, s * P : (s + 1) * P], src, ident[:])
+            st[key, "bank"] = bank
+
+        def gather(key, copy=nc.scalar.copy):
+            grouped = deep.tile([P, 2 * K_PASS], BF16, name="grouped", tag="grouped", align_bytes=64, bufs=4)
+            copy(
+                out=grouped[:].bitcast(F32).rearrange("p (g r u) -> p g r u", g=2, u=2),
+                in_=st[key, "bank"][:].rearrange("p (g u r) -> p g r u", g=2, u=2),
+            )
+            st[key, "grouped"] = grouped
+
+        def quantize(key):
+            codes = deep.tile([P, 2 * P], U32, name="codes", tag="codes", align_bytes=64, bufs=6)
+            scales = deep.tile([P, 2 * P], U8, name="scales", tag="scales", align_bytes=64, bufs=6)
+            nc.vector.quantize_mx(out=codes[:].bitcast(FP8X4), scales=scales[:], in_=st[key, "grouped"][:])
+            st[key, "mx"] = (codes, scales)
+
+        def mx_pass(bank, key, g, w, ws, wg, c, start, stop):
+            codes, scales = st[key, "mx"]
+            nc.tensor.matmul_mx(
+                out=bank[:],
+                lhsT=codes[:, g * P : (g + 1) * P].bitcast(FP8X4),
+                lhsT_scale=scales[:, g * P : (g + 1) * P],
+                rhs=w[c][:, wg, :].bitcast(FP4X4),
+                rhs_scale=ws[:, wg, c * BANK : (c + 1) * BANK],
+                start=start,
+                stop=stop,
+            )
+
+        def turn_x(j):
+            words = xs[j][:].bitcast(F32)
+            turn(("x", j), [words[:, 256 * g + u : 256 * (g + 1) : 2] for g in range(GC) for u in range(2)])
+
+        def stage1(j, c):
+            bank = next_bank()
+            for g in range(GC):
+                mx_pass(bank, ("x", j), g, w1, w1s, g, c, g == 0, g == GC - 1)
+            st["z", j, c] = bank
+
+        def gelu(j, c):
+            if c % 2 == 0:
+                act = deep.tile([P, 2 * BANK], F32, name="act", tag="act", align_bytes=64)
+                st["act", j, c // 2] = act
+            act = st["act", j, c // 2]
+            nc.scalar.activation(
+                out=act[:, (c % 2) * BANK : (c % 2 + 1) * BANK].rearrange("p (u q e) -> p u q e", u=2, e=2),
+                in_=st["z", j, c][:].rearrange("p (q u e) -> p u q e", u=2, e=2),
+                func=ACT.Gelu_apprx_tanh,
+            )
+
+        def scale_hidden(j, h):
+            hid = deep.tile([P, 2 * BANK], BF16, name="hid", tag="hid", align_bytes=64, bufs=4)
+            nc.vector.tensor_tensor(out=hid[:], in0=st["act", j, h][:], in1=hs_banks[h][:].bitcast(BF16), op=ALU.mult)
+            st["hid", j, h] = hid
+
+        def turn_h(j, h):
+            words = st["hid", j, h][:].bitcast(F32)
+            turn(("h", j, h), [words[:, s * P : (s + 1) * P] for s in range(4)])
+
+        def stage2(j, n):
+            bank = next_bank()
+            for g in range(GF):
+                mx_pass(bank, ("h", j, g // 2), g % 2, w2, w2s, g, n, g == 0, g == GF - 1)
+            st["o", j, n] = bank
+
+        def residual(j):
+            res = deep.tile([P, C], F32, name="res", tag="res", align_bytes=64)
+            for n in range(GC):
+                cols = slice(n * BANK, (n + 1) * BANK)
+                nc.gpsimd.tensor_tensor(out=res[:, cols], in0=skips[j][:, cols], in1=osb_all[:, cols], op=ALU.add)
+            st["res", j] = res
+
+        def scale_out(j, n):
+            if n == 0:
+                branch = work.tile([P, C], F32, name="branch", tag="branch", align_bytes=64)
+                st["branch", j] = branch
+            cols = slice(n * BANK, (n + 1) * BANK)
+            nc.vector.tensor_tensor(out=st["branch", j][:, cols], in0=st["o", j, n][:], in1=os_all[:, cols], op=ALU.mult)
+
+        def add_out(j, halves):
+            if halves[0] == 0:
+                y = deep.tile([P, C], F32, name="y", tag="y", align_bytes=64)
+                st["y", j] = y
+            cols = slice(halves[0] * BANK, (halves[-1] + 1) * BANK)
+            y = st["y", j]
+            nc.vector.tensor_tensor(out=y[:, cols], in0=st["branch", j][:, cols], in1=st["res", j][:, cols], op=ALU.add)
+            nc.sync.dma_start(out=y_rows[j * P : (j + 1) * P, cols], in_=y[:, cols])
+
+        def round_y(j, g):
+            if g == 0:
+                y16 = work.tile([P, C], BF16, name="y16", tag="y16", align_bytes=64)
+                st["y16", j] = y16
+            cols = slice(g * BANK, (g + 1) * BANK)
+            nc.scalar.copy(
+                out=st["y16", j][:, cols].rearrange("p (u q e) -> p u q e", u=2, e=2),
+                in_=st["y", j][:, cols].rearrange("p (q u e) -> p u q e", u=2, e=2),
+            )
+
+        def turn_y(j):
+            words = st["y16", j][:].bitcast(F32)
+            turn(("y", j), [words[:, s * P : (s + 1) * P] for s in range(4)])
+
+        def quantize_y(j):
+            for g in range(GC):
+                nc.vector.quantize_mx(
+                    out=y_codes[:, g, j * P : (j + 1) * P].bitcast(FP8X4),
+                    scales=y_scales[:, g, j * P : (j + 1) * P],
+                    in_=st[("y", j), "grouped"][:, g * K_PASS : (g + 1) * K_PASS],
+                )
+            nc.sync.dma_start(
+                out=words_out[:, :, 4 * P * j : 4 * P * (j + 1)].bitcast(I32),
+                in_=y_codes[:, :, j * P : (j + 1) * P].bitcast(I32),
+            )
+
+        def store_scales(first, last, queues):
+            cols = slice(first * P, last * P)
+            for q in range(4):
+                queues[q % len(queues)].dma_start(
+                    out=out_2[:, 4 * q : 4 * q + 4, cols].rearrange("g r m -> r g m").bitcast(I32),
+                    in_=y_scales[32 * q : 32 * q + 4, :, cols].bitcast(I32),
+                )
+
+        def round_last(j, g, direct):
+            cols = slice(g * BANK, (g + 1) * BANK)
+            y16 = work.tile([P, BANK], BF16, name="y16_last", tag="y16_last", align_bytes=64)
+            word_order = y16[:].rearrange("p (u q e) -> p u q e", u=2, e=2)
+            if direct:
+                nc.vector.tensor_tensor(
+                    out=word_order,
+                    in0=st["branch", j][:, cols].rearrange("p (q u e) -> p u q e", u=2, e=2),
+                    in1=st["res", j][:, cols].rearrange("p (q u e) -> p u q e", u=2, e=2),
+                    op=ALU.add,
+                )
+            else:
+                nc.scalar.copy(out=word_order, in_=st["y", j][:, cols].rearrange("p (q u e) -> p u q e", u=2, e=2))
+            st["y16_last", g] = y16
+
+        def turn_last(g):
+            words = st["y16_last", g][:].bitcast(F32)
+            bank = next_bank()
+            for u in range(2):
+                nc.tensor.transpose(bank[:, u * P : (u + 1) * P], words[:, u * P : (u + 1) * P], ident[:])
+            grouped = work.tile([P, K_PASS], BF16, name="grouped_last", tag="grouped_last", align_bytes=64)
+            nc.scalar.copy(
+                out=grouped[:].bitcast(F32).rearrange("p (r u) -> p r u", u=2),
+                in_=bank[:, 0 : 2 * P].rearrange("p (u r) -> p r u", u=2),
+            )
+            st["last", g] = grouped
+
+        def quantize_last(j, g):
+            nc.vector.quantize_mx(
+                out=y_codes[:, g, j * P : (j + 1) * P].bitcast(FP8X4),
+                scales=y_scales[:, g, j * P : (j + 1) * P],
+                in_=st["last", g][:],
+            )
+
+        def store_words(j):
+            nc.sync.dma_start(
+                out=words_out[:, :, 4 * P * j : 4 * P * (j + 1)].bitcast(I32),
+                in_=y_codes[:, :, j * P : (j + 1) * P].bitcast(I32),
+            )
+
+        def live(j):
+            return 0 <= j < TILES
+
+        spread_channels(os_rows, os_all)
+        turn_x(0)
+        gather(("x", 0))
+        quantize(("x", 0))
+        spread_hidden(0)
+        spread_hidden(1)
+        for c in range(2):
+            stage1(0, c)
+            gelu(0, c)
+        turn_x(1)
+        spread_channels(b2_rows, b2_all)
+        gather(("x", 1), nc.vector.tensor_copy)
+        for c in range(2, GF):
+            stage1(0, c)
+            gelu(0, c)
+        scale_hidden(0, 0)
+        quantize(("x", 1))
+        turn_x(2)
+        gather(("x", 2), nc.vector.tensor_copy)
+        scale_hidden(0, 1)
+        quantize(("x", 2))
+        nc.vector.tensor_tensor(out=osb_all[:], in0=os_all[:], in1=b2_all[:], op=ALU.mult)
+        for c in range(GF):
+            stage1(1, c)
+            gelu(1, c)
+        residual(0)
+        scale_hidden(1, 0)
+        scale_hidden(1, 1)
+
+        last = TILES - 1
+        for i in range(2, TILES):
+            turn_h(i - 2, 0)
+            turn_h(i - 2, 1)
+            if live(i + 1):
+                turn_x(i + 1)
+            if live(i - 4):
+                turn_y(i - 4)
+            gather(("h", i - 2, 0))
+            gather(("h", i - 2, 1))
+            if live(i + 1):
+                gather(("x", i + 1))
+            if live(i - 4):
+                gather(("y", i - 4))
+            quantize(("h", i - 2, 0))
+            quantize(("h", i - 2, 1))
+            if live(i + 1):
+                quantize(("x", i + 1))
+            if live(i - 4):
+                quantize_y(i - 4)
+            if live(i - 3):
+                add_out(i - 3, [0, 1])
+                residual(i)
+            else:
+                residual(1)
+                residual(2)
+            for c in range(GF):
+                stage1(i, c)
+                gelu(i, c)
+            if i == last:
+                turn_h(last - 1, 0)
+                turn_h(last - 1, 1)
+                gather(("h", last - 1, 0))
+                gather(("h", last - 1, 1))
+            if live(i - 3):
+                round_y(i - 3, 0)
+                round_y(i - 3, 1)
+            stage2(i - 2, 0)
+            stage2(i - 2, 1)
+            scale_hidden(i, 0)
+            scale_hidden(i, 1)
+            if i == last:
+                quantize(("h", last - 1, 0))
+                quantize(("h", last - 1, 1))
+            scale_out(i - 2, 0)
+            scale_out(i - 2, 1)
+
+        turn_h(last, 0)
+        turn_h(last, 1)
+        turn_y(last - 3)
+        gather(("h", last, 0))
+        gather(("h", last, 1))
+        gather(("y", last - 3))
+        quantize(("h", last, 0))
+        add_out(last - 2, [0, 1])
+        quantize(("h", last, 1))
+        round_y(last - 2, 0)
+        round_y(last - 2, 1)
+        stage2(last - 1, 0)
+        stage2(last - 1, 1)
+        scale_out(last - 1, 0)
+        quantize_y(last - 3)
+        scale_out(last - 1, 1)
+        turn_y(last - 2)
+        gather(("y", last - 2))
+        add_out(last - 1, [0])
+        round_y(last - 1, 0)
+        stage2(last, 0)
+        add_out(last - 1, [1])
+        round_y(last - 1, 1)
+        stage2(last, 1)
+        scale_out(last, 0)
+        quantize_y(last - 2)
+        store_scales(0, last - 1, [nc.sync])
+        add_out(last, [0])
+        round_last(last, 0, False)
+        turn_y(last - 1)
+        gather(("y", last - 1))
+        turn_last(0)
+        scale_out(last, 1)
+        round_last(last, 1, True)
+        quantize_y(last - 1)
+        turn_last(1)
+        add_out(last, [1])
+        quantize_last(last, 0)
+        quantize_last(last, 1)
+        store_words(last)
+        store_scales(last - 1, TILES, [nc.scalar, nc.sync])

@@ -23,6 +23,7 @@ TILES = TOKENS // P
 GC = C // K_PASS
 GF = F // K_PASS
 RING_BANKS = 6
+EARLY_TILES = TILES - 3
 
 
 def tile_scaled_mixer_channel_mixing_h1_kernel(
@@ -60,11 +61,13 @@ def tile_scaled_mixer_channel_mixing_h1_kernel(
         os_rows = keep.tile([P, C // P], BF16, name="os_rows")
         b2_rows = keep.tile([P, C // P], BF16, name="b2_rows")
         hs_banks = [psum.tile([P, BANK], F32, name="hs_bank%d" % h) for h in range(2)]
+        hs_first = keep.tile([P, BANK], BF16, name="hs_first", align_bytes=64)
         os_all = keep.tile([P, C], BF16, name="os_all", align_bytes=64)
         b2_all = keep.tile([P, C], BF16, name="b2_all", align_bytes=64)
         osb_all = keep.tile([P, C], F32, name="osb_all", align_bytes=64)
-        y_codes = keep.tile([P, GC, TOKENS], U32, name="y_codes", align_bytes=64)
-        y_scales = keep.tile([P, GC, TOKENS], U8, name="y_scales", align_bytes=64)
+        y_codes = keep.tile([P, TILES, GC, P], U32, name="y_codes", align_bytes=64)
+        y_scales = keep.tile([P, EARLY_TILES, GC, P], U8, name="y_scales", align_bytes=64)
+        late_scales = keep.tile([P, GC, TILES - EARLY_TILES, P], U8, name="late_scales", align_bytes=64)
         warm = keep.tile([P, 1], F32, name="warm")
 
         def load_rows(dst, rows, j):
@@ -74,35 +77,39 @@ def tile_scaled_mixer_channel_mixing_h1_kernel(
             src = words.rearrange("g p n -> p g n")[:, :, 2 * BANK * c : 2 * BANK * (c + 1)]
             nc.sync.dma_start(out=dst[c][:].bitcast(I32), in_=src.bitcast(I32))
 
-        def load_scales(dst, scales):
+        def load_scales(dst, scales, lo, hi):
             for q in range(4):
-                src = scales[:, 4 * q : 4 * q + 4, :].rearrange("g r n -> r g n")
-                nc.sync.dma_start(out=dst[32 * q : 32 * q + 4, :, :].bitcast(I32), in_=src.bitcast(I32))
+                src = scales[:, 4 * q : 4 * q + 4, lo:hi].rearrange("g r n -> r g n")
+                nc.sync.dma_start(out=dst[32 * q : 32 * q + 4, :, lo:hi].bitcast(I32), in_=src.bitcast(I32))
 
+        nc.scalar.dma_start(out=os_rows[:], in_=out_scale.rearrange("(p k) -> p k", p=P))
+        nc.scalar.dma_start(out=b2_rows[:], in_=b2.rearrange("(p k) -> p k", p=P))
         nc.vector.memset(w1s[:].bitcast(I32), 0)
         nc.vector.memset(w2s[:].bitcast(I32), 0)
         make_identity(nc, ident[:])
-        nc.scalar.dma_start(out=os_rows[:], in_=out_scale.rearrange("(p k) -> p k", p=P))
-        nc.scalar.dma_start(out=hs_rows[:], in_=hid_scale.rearrange("(g p k) -> p g k", g=GF, p=P))
-        nc.scalar.dma_start(out=b2_rows[:], in_=b2.rearrange("(p k) -> p k", p=P))
         nc.scalar.activation(out=warm[:], in_=ident[:, 0:1], func=ACT.Gelu_apprx_tanh)
 
         load_rows(xs, x_rows, 0)
-        load_scales(w1s, w1_scales)
+        load_scales(w1s, w1_scales, 0, F // 2)
         load_words(w1, w1_words, 0)
+        nc.sync.dma_start(out=hs_rows[:], in_=hid_scale.rearrange("(g p k) -> p g k", g=GF, p=P))
         load_words(w1, w1_words, 1)
         load_rows(xs, x_rows, 1)
+        load_scales(w1s, w1_scales, F // 2, F)
         load_words(w1, w1_words, 2)
         load_words(w1, w1_words, 3)
         load_rows(xs, x_rows, 2)
-        load_scales(w2s, w2_scales)
-        load_words(w2, w2_words, 0)
+        load_rows(skips, skip_rows, 0)
+        load_rows(skips, skip_rows, 1)
+        load_scales(w2s, w2_scales, 0, C)
         load_rows(xs, x_rows, 3)
+        load_words(w2, w2_words, 0)
+        load_rows(skips, skip_rows, 2)
         load_words(w2, w2_words, 1)
-        for j in range(TILES):
-            load_rows(skips, skip_rows, j)
-            if j + 4 < TILES:
-                load_rows(xs, x_rows, j + 4)
+        for j in range(4, TILES):
+            load_rows(xs, x_rows, j)
+            load_rows(skips, skip_rows, j - 1)
+        load_rows(skips, skip_rows, TILES - 1)
 
         st = {}
 
@@ -122,34 +129,43 @@ def tile_scaled_mixer_channel_mixing_h1_kernel(
             words = hs_rows[:].rearrange("p g k -> p (g k)").bitcast(F32)
             spread(hs_banks[h], words[:, 4 * h : 4 * h + 4])
 
-        def turn(key, sources):
+        def turn(key, sources, part=0):
             bank = next_bank()
             for s, src in enumerate(sources):
                 nc.tensor.transpose(bank[:, s * P : (s + 1) * P], src, ident[:])
-            st[key, "bank"] = bank
+            st[key, "bank", part] = bank
 
-        def gather(key, copy=nc.scalar.copy):
-            grouped = deep.tile([P, 2 * K_PASS], BF16, name="grouped", tag="grouped", align_bytes=64, bufs=4)
+        def gather(key, part=0, copy=nc.scalar.copy):
+            if part == 0:
+                grouped = deep.tile([P, F], BF16, name="grouped", tag="grouped", align_bytes=64, bufs=5)
+                st[key, "grouped"] = grouped
+            dst = st[key, "grouped"][:, part * 2 * K_PASS : (part + 1) * 2 * K_PASS]
             copy(
-                out=grouped[:].bitcast(F32).rearrange("p (g r u) -> p g r u", g=2, u=2),
-                in_=st[key, "bank"][:].rearrange("p (g u r) -> p g r u", g=2, u=2),
+                out=dst.bitcast(F32).rearrange("p (g r u) -> p g r u", g=2, u=2),
+                in_=st[key, "bank", part][:].rearrange("p (g u r) -> p g r u", g=2, u=2),
             )
-            st[key, "grouped"] = grouped
 
-        def quantize(key):
-            codes = deep.tile([P, 2 * P], U32, name="codes", tag="codes", align_bytes=64, bufs=6)
-            scales = deep.tile([P, 2 * P], U8, name="scales", tag="scales", align_bytes=64, bufs=6)
-            nc.vector.quantize_mx(out=codes[:].bitcast(FP8X4), scales=scales[:], in_=st[key, "grouped"][:])
-            st[key, "mx"] = (codes, scales)
+        def quantize(key, groups):
+            if groups[0] == 0:
+                codes = deep.tile([P, GF * P], U32, name="codes", tag="codes", align_bytes=64, bufs=4)
+                scales = deep.tile([P, GF * P], U8, name="scales", tag="scales", align_bytes=64, bufs=4)
+                st[key, "mx"] = (codes, scales)
+            codes, scales = st[key, "mx"]
+            lo, hi = groups[0], groups[-1] + 1
+            nc.vector.quantize_mx(
+                out=codes[:, lo * P : hi * P].bitcast(FP8X4),
+                scales=scales[:, lo * P : hi * P],
+                in_=st[key, "grouped"][:, lo * K_PASS : hi * K_PASS],
+            )
 
-        def mx_pass(bank, key, g, w, ws, wg, c, start, stop):
+        def mx_pass(bank, key, g, w, ws, c, start, stop):
             codes, scales = st[key, "mx"]
             nc.tensor.matmul_mx(
                 out=bank[:],
                 lhsT=codes[:, g * P : (g + 1) * P].bitcast(FP8X4),
                 lhsT_scale=scales[:, g * P : (g + 1) * P],
-                rhs=w[c][:, wg, :].bitcast(FP4X4),
-                rhs_scale=ws[:, wg, c * BANK : (c + 1) * BANK],
+                rhs=w[c][:, g, :].bitcast(FP4X4),
+                rhs_scale=ws[:, g, c * BANK : (c + 1) * BANK],
                 start=start,
                 stop=stop,
             )
@@ -161,12 +177,12 @@ def tile_scaled_mixer_channel_mixing_h1_kernel(
         def stage1(j, c):
             bank = next_bank()
             for g in range(GC):
-                mx_pass(bank, ("x", j), g, w1, w1s, g, c, g == 0, g == GC - 1)
+                mx_pass(bank, ("x", j), g, w1, w1s, c, g == 0, g == GC - 1)
             st["z", j, c] = bank
 
         def gelu(j, c):
             if c % 2 == 0:
-                act = deep.tile([P, 2 * BANK], F32, name="act", tag="act", align_bytes=64)
+                act = deep.tile([P, 2 * BANK], F32, name="act", tag="act", align_bytes=64, bufs=4)
                 st["act", j, c // 2] = act
             act = st["act", j, c // 2]
             nc.scalar.activation(
@@ -175,27 +191,41 @@ def tile_scaled_mixer_channel_mixing_h1_kernel(
                 func=ACT.Gelu_apprx_tanh,
             )
 
-        def scale_hidden(j, h):
-            hid = deep.tile([P, 2 * BANK], BF16, name="hid", tag="hid", align_bytes=64, bufs=4)
-            nc.vector.tensor_tensor(out=hid[:], in0=st["act", j, h][:], in1=hs_banks[h][:].bitcast(BF16), op=ALU.mult)
-            st["hid", j, h] = hid
+        def hidden_tile(j, h):
+            if ("hid", j, h) not in st:
+                hid = deep.tile([P, 2 * BANK], BF16, name="hid", tag="hid", align_bytes=64, bufs=4)
+                st["hid", j, h] = hid
+            return st["hid", j, h]
+
+        def scale_hidden(j, h, lo=0):
+            nc.vector.tensor_tensor(
+                out=hidden_tile(j, h)[:, lo:], in0=st["act", j, h][:, lo:], in1=hs_banks[h][:].bitcast(BF16)[:, lo:], op=ALU.mult
+            )
+
+        def scale_first_chunk(j):
+            nc.gpsimd.tensor_tensor(
+                out=hidden_tile(j, 0)[:, 0:BANK], in0=st["act", j, 0][:, 0:BANK], in1=hs_first[:], op=ALU.mult
+            )
+
+        def keep_first_chunk():
+            nc.vector.tensor_copy(out=hs_first[:].bitcast(F32), in_=hs_banks[0][:, 0 : BANK // 2])
 
         def turn_h(j, h):
             words = st["hid", j, h][:].bitcast(F32)
-            turn(("h", j, h), [words[:, s * P : (s + 1) * P] for s in range(4)])
+            turn(("h", j), [words[:, s * P : (s + 1) * P] for s in range(4)], h)
 
         def stage2(j, n):
             bank = next_bank()
             for g in range(GF):
-                mx_pass(bank, ("h", j, g // 2), g % 2, w2, w2s, g, n, g == 0, g == GF - 1)
+                mx_pass(bank, ("h", j), g, w2, w2s, n, g == 0, g == GF - 1)
             st["o", j, n] = bank
 
-        def residual(j):
-            res = deep.tile([P, C], F32, name="res", tag="res", align_bytes=64)
-            for n in range(GC):
-                cols = slice(n * BANK, (n + 1) * BANK)
-                nc.gpsimd.tensor_tensor(out=res[:, cols], in0=skips[j][:, cols], in1=osb_all[:, cols], op=ALU.add)
-            st["res", j] = res
+        def residual(j, n):
+            if ("res", j) not in st:
+                res = deep.tile([P, C], F32, name="res", tag="res", align_bytes=64)
+                st["res", j] = res
+            cols = slice(n * BANK, (n + 1) * BANK)
+            nc.gpsimd.tensor_tensor(out=st["res", j][:, cols], in0=skips[j][:, cols], in1=osb_all[:, cols], op=ALU.add)
 
         def scale_out(j, n):
             if n == 0:
@@ -204,47 +234,59 @@ def tile_scaled_mixer_channel_mixing_h1_kernel(
             cols = slice(n * BANK, (n + 1) * BANK)
             nc.vector.tensor_tensor(out=st["branch", j][:, cols], in0=st["o", j, n][:], in1=os_all[:, cols], op=ALU.mult)
 
-        def add_out(j, halves):
-            if halves[0] == 0:
+        def add_out(j, lo, hi, engine=nc.vector):
+            if ("y", j) not in st:
                 y = deep.tile([P, C], F32, name="y", tag="y", align_bytes=64)
                 st["y", j] = y
-            cols = slice(halves[0] * BANK, (halves[-1] + 1) * BANK)
             y = st["y", j]
-            nc.vector.tensor_tensor(out=y[:, cols], in0=st["branch", j][:, cols], in1=st["res", j][:, cols], op=ALU.add)
-            nc.sync.dma_start(out=y_rows[j * P : (j + 1) * P, cols], in_=y[:, cols])
+            engine.tensor_tensor(out=y[:, lo:hi], in0=st["branch", j][:, lo:hi], in1=st["res", j][:, lo:hi], op=ALU.add)
 
-        def round_y(j, g):
-            if g == 0:
-                y16 = work.tile([P, C], BF16, name="y16", tag="y16", align_bytes=64)
-                st["y16", j] = y16
-            cols = slice(g * BANK, (g + 1) * BANK)
+        def store_y(j, lo, hi):
+            nc.sync.dma_start(out=y_rows[j * P : (j + 1) * P, lo:hi], in_=st["y", j][:, lo:hi])
+
+        def round_y(j):
+            y16 = work.tile([P, C], BF16, name="y16", tag="y16", align_bytes=64)
             nc.scalar.copy(
-                out=st["y16", j][:, cols].rearrange("p (u q e) -> p u q e", u=2, e=2),
-                in_=st["y", j][:, cols].rearrange("p (q u e) -> p u q e", u=2, e=2),
+                out=y16[:].rearrange("p (u q e) -> p u q e", u=2, e=2),
+                in_=st["y", j][:].rearrange("p (q u e) -> p u q e", u=2, e=2),
             )
+            st["y16", j] = y16
 
         def turn_y(j):
             words = st["y16", j][:].bitcast(F32)
-            turn(("y", j), [words[:, s * P : (s + 1) * P] for s in range(4)])
+            turn(("y", j), [words[:, (GC * u + g) * P : (GC * u + g + 1) * P] for g in range(GC) for u in range(2)])
 
-        def quantize_y(j):
-            for g in range(GC):
-                nc.vector.quantize_mx(
-                    out=y_codes[:, g, j * P : (j + 1) * P].bitcast(FP8X4),
-                    scales=y_scales[:, g, j * P : (j + 1) * P],
-                    in_=st[("y", j), "grouped"][:, g * K_PASS : (g + 1) * K_PASS],
-                )
+        def store_words(j):
             nc.sync.dma_start(
-                out=words_out[:, :, 4 * P * j : 4 * P * (j + 1)].bitcast(I32),
-                in_=y_codes[:, :, j * P : (j + 1) * P].bitcast(I32),
+                out=words_out[:, :, 4 * P * j : 4 * P * (j + 1)].bitcast(I32), in_=y_codes[:, j, :, :].bitcast(I32)
             )
 
-        def store_scales(first, last, queues):
-            cols = slice(first * P, last * P)
+        def quantize_y(j):
+            nc.vector.quantize_mx(
+                out=y_codes[:, j, :, :].rearrange("p g m -> p (g m)").bitcast(FP8X4),
+                scales=y_scales[:, j, :, :].rearrange("p g m -> p (g m)"),
+                in_=st[("y", j), "grouped"][:, 0:C],
+            )
+            store_words(j)
+
+        def quantize_late(j, g, grouped):
+            nc.vector.quantize_mx(
+                out=y_codes[:, j, g, :].bitcast(FP8X4), scales=late_scales[:, g, j - EARLY_TILES, :], in_=grouped
+            )
+
+        def store_early_scales():
+            for q in range(4):
+                for g in range(GC):
+                    nc.sync.dma_start(
+                        out=out_2[g, 4 * q : 4 * q + 4, 0 : EARLY_TILES * P].rearrange("r (j m) -> r j m", m=P).bitcast(I32),
+                        in_=y_scales[32 * q : 32 * q + 4, :, g, :].bitcast(I32),
+                    )
+
+        def store_late_scales(queues):
             for q in range(4):
                 queues[q % len(queues)].dma_start(
-                    out=out_2[:, 4 * q : 4 * q + 4, cols].rearrange("g r m -> r g m").bitcast(I32),
-                    in_=y_scales[32 * q : 32 * q + 4, :, cols].bitcast(I32),
+                    out=out_2[:, 4 * q : 4 * q + 4, EARLY_TILES * P : TOKENS].rearrange("g r m -> r g m").bitcast(I32),
+                    in_=late_scales[32 * q : 32 * q + 4, :, :, :].rearrange("r g j m -> r g (j m)").bitcast(I32),
                 )
 
         def round_last(j, g, direct):
@@ -262,148 +304,169 @@ def tile_scaled_mixer_channel_mixing_h1_kernel(
                 nc.scalar.copy(out=word_order, in_=st["y", j][:, cols].rearrange("p (q u e) -> p u q e", u=2, e=2))
             st["y16_last", g] = y16
 
-        def turn_last(g):
-            words = st["y16_last", g][:].bitcast(F32)
+        def turn_half(key, g, sources):
             bank = next_bank()
-            for u in range(2):
-                nc.tensor.transpose(bank[:, u * P : (u + 1) * P], words[:, u * P : (u + 1) * P], ident[:])
-            grouped = work.tile([P, K_PASS], BF16, name="grouped_last", tag="grouped_last", align_bytes=64)
+            for u, src in enumerate(sources):
+                nc.tensor.transpose(bank[:, u * P : (u + 1) * P], src, ident[:])
+            if g == 0:
+                grouped = deep.tile([P, F], BF16, name="grouped", tag="grouped", align_bytes=64, bufs=5)
+                st[key, "grouped"] = grouped
             nc.scalar.copy(
-                out=grouped[:].bitcast(F32).rearrange("p (r u) -> p r u", u=2),
+                out=st[key, "grouped"][:, g * K_PASS : (g + 1) * K_PASS].bitcast(F32).rearrange("p (r u) -> p r u", u=2),
                 in_=bank[:, 0 : 2 * P].rearrange("p (u r) -> p r u", u=2),
             )
-            st["last", g] = grouped
 
-        def quantize_last(j, g):
-            nc.vector.quantize_mx(
-                out=y_codes[:, g, j * P : (j + 1) * P].bitcast(FP8X4),
-                scales=y_scales[:, g, j * P : (j + 1) * P],
-                in_=st["last", g][:],
-            )
+        def turn_first(g):
+            words = xs[0][:].bitcast(F32)
+            turn_half(("x", 0), g, [words[:, 256 * g + u : 256 * (g + 1) : 2] for u in range(2)])
 
-        def store_words(j):
-            nc.sync.dma_start(
-                out=words_out[:, :, 4 * P * j : 4 * P * (j + 1)].bitcast(I32),
-                in_=y_codes[:, :, j * P : (j + 1) * P].bitcast(I32),
-            )
+        def turn_last(g):
+            words = st["y16_last", g][:].bitcast(F32)
+            turn_half(("y", TILES - 1), g, [words[:, u * P : (u + 1) * P] for u in range(2)])
+
+        def quantize_late_y(j, g):
+            quantize_late(j, g, st[("y", j), "grouped"][:, g * K_PASS : (g + 1) * K_PASS])
 
         def live(j):
             return 0 <= j < TILES
 
         spread_channels(os_rows, os_all)
-        turn_x(0)
-        gather(("x", 0))
-        quantize(("x", 0))
-        spread_hidden(0)
-        spread_hidden(1)
+        turn_first(0)
+        turn_first(1)
+        quantize(("x", 0), [0])
+        quantize(("x", 0), [1])
+        spread_channels(b2_rows, b2_all)
+        nc.vector.tensor_tensor(out=osb_all[:], in0=os_all[:], in1=b2_all[:], op=ALU.mult)
         for c in range(2):
             stage1(0, c)
             gelu(0, c)
         turn_x(1)
-        spread_channels(b2_rows, b2_all)
-        gather(("x", 1), nc.vector.tensor_copy)
+        spread_hidden(0)
+        gather(("x", 1), copy=nc.vector.tensor_copy)
+        keep_first_chunk()
+        quantize(("x", 1), [0, 1])
         for c in range(2, GF):
             stage1(0, c)
             gelu(0, c)
         scale_hidden(0, 0)
-        quantize(("x", 1))
         turn_x(2)
-        gather(("x", 2), nc.vector.tensor_copy)
+        spread_hidden(1)
+        gather(("x", 2), copy=nc.vector.tensor_copy)
         scale_hidden(0, 1)
-        quantize(("x", 2))
-        nc.vector.tensor_tensor(out=osb_all[:], in0=os_all[:], in1=b2_all[:], op=ALU.mult)
+        quantize(("x", 2), [0, 1])
         for c in range(GF):
             stage1(1, c)
             gelu(1, c)
-        residual(0)
-        scale_hidden(1, 0)
+        residual(0, 0)
+        residual(0, 1)
+        scale_first_chunk(1)
+        residual(1, 0)
+        residual(1, 1)
+        scale_hidden(1, 0, BANK)
         scale_hidden(1, 1)
 
         last = TILES - 1
-        for i in range(2, TILES):
+        for i in range(2, last):
             turn_h(i - 2, 0)
             turn_h(i - 2, 1)
-            if live(i + 1):
-                turn_x(i + 1)
+            turn_x(i + 1)
             if live(i - 4):
                 turn_y(i - 4)
-            gather(("h", i - 2, 0))
-            gather(("h", i - 2, 1))
-            if live(i + 1):
-                gather(("x", i + 1))
+            gather(("h", i - 2), 0)
+            gather(("h", i - 2), 1)
+            gather(("x", i + 1))
             if live(i - 4):
                 gather(("y", i - 4))
-            quantize(("h", i - 2, 0))
-            quantize(("h", i - 2, 1))
-            if live(i + 1):
-                quantize(("x", i + 1))
-            if live(i - 4):
-                quantize_y(i - 4)
+            if live(i - 5):
+                quantize_y(i - 5)
+            quantize(("h", i - 2), [0, 1, 2, 3])
+            quantize(("x", i + 1), [0, 1])
             if live(i - 3):
-                add_out(i - 3, [0, 1])
-                residual(i)
-            else:
-                residual(1)
-                residual(2)
+                add_out(i - 3, 0, C)
+                store_y(i - 3, 0, C)
             for c in range(GF):
                 stage1(i, c)
                 gelu(i, c)
-            if i == last:
-                turn_h(last - 1, 0)
-                turn_h(last - 1, 1)
-                gather(("h", last - 1, 0))
-                gather(("h", last - 1, 1))
+            residual(i, 0)
+            residual(i, 1)
+            scale_first_chunk(i)
             if live(i - 3):
-                round_y(i - 3, 0)
-                round_y(i - 3, 1)
+                round_y(i - 3)
             stage2(i - 2, 0)
             stage2(i - 2, 1)
-            scale_hidden(i, 0)
+            scale_hidden(i, 0, BANK)
             scale_hidden(i, 1)
-            if i == last:
-                quantize(("h", last - 1, 0))
-                quantize(("h", last - 1, 1))
             scale_out(i - 2, 0)
             scale_out(i - 2, 1)
 
-        turn_h(last, 0)
-        turn_h(last, 1)
-        turn_y(last - 3)
-        gather(("h", last, 0))
-        gather(("h", last, 1))
-        gather(("y", last - 3))
-        quantize(("h", last, 0))
-        add_out(last - 2, [0, 1])
-        quantize(("h", last, 1))
-        round_y(last - 2, 0)
-        round_y(last - 2, 1)
-        stage2(last - 1, 0)
-        stage2(last - 1, 1)
-        scale_out(last - 1, 0)
-        quantize_y(last - 3)
-        scale_out(last - 1, 1)
-        turn_y(last - 2)
-        gather(("y", last - 2))
-        add_out(last - 1, [0])
-        round_y(last - 1, 0)
-        stage2(last, 0)
-        add_out(last - 1, [1])
-        round_y(last - 1, 1)
-        stage2(last, 1)
-        scale_out(last, 0)
-        quantize_y(last - 2)
-        store_scales(0, last - 1, [nc.sync])
-        add_out(last, [0])
-        round_last(last, 0, False)
-        turn_y(last - 1)
-        gather(("y", last - 1))
+        a, b, z = last - 2, last - 1, last
+        turn_h(a, 0)
+        turn_h(a, 1)
+        gather(("h", a), 0)
+        gather(("h", a), 1)
+        quantize_y(a - 3)
+        quantize(("h", a), [0, 1, 2, 3])
+        add_out(a - 1, 0, C)
+        store_y(a - 1, 0, C)
+        for c in range(GF):
+            stage1(z, c)
+            gelu(z, c)
+        residual(z, 0)
+        residual(z, 1)
+        scale_hidden(z, 0)
+        stage2(a, 0)
+        turn_h(b, 0)
+        turn_h(b, 1)
+        round_y(a - 1)
+        gather(("h", b), 0)
+        gather(("h", b), 1)
+        scale_out(a, 0)
+        scale_hidden(z, 1)
+        stage2(a, 1)
+        turn_y(a - 2)
+        turn_y(a - 1)
+        turn_h(z, 0)
+        turn_h(z, 1)
+        quantize(("h", b), [0, 1, 2, 3])
+        scale_out(a, 1)
+        gather(("y", a - 2))
+        gather(("y", a - 1))
+        gather(("h", z), 0)
+        gather(("h", z), 1)
+        quantize_y(a - 2)
+        add_out(a, 0, C)
+        store_y(a, 0, C)
+        round_y(a)
+        stage2(b, 0)
+        stage2(b, 1)
+        quantize_y(a - 1)
+        store_early_scales()
+        quantize(("h", z), [0, 1])
+        scale_out(b, 0)
+        quantize(("h", z), [2, 3])
+        scale_out(b, 1)
+        stage2(z, 0)
+        stage2(z, 1)
+        add_out(b, 0, BANK)
+        add_out(b, BANK, C)
+        store_y(b, 0, C)
+        round_y(b)
+        scale_out(z, 0)
+        scale_out(z, 1)
+        add_out(z, 0, BANK)
+        store_y(z, 0, BANK)
+        turn_y(a)
+        gather(("y", a))
+        round_last(z, 0, False)
+        round_last(z, 1, True)
+        add_out(z, BANK, C)
+        store_y(z, BANK, C)
+        turn_y(b)
+        gather(("y", b))
         turn_last(0)
-        scale_out(last, 1)
-        round_last(last, 1, True)
-        quantize_y(last - 1)
         turn_last(1)
-        add_out(last, [1])
-        quantize_last(last, 0)
-        quantize_last(last, 1)
-        store_words(last)
-        store_scales(last - 1, TILES, [nc.scalar, nc.sync])
+        for j in (a, b, z):
+            quantize_late_y(j, 0)
+            quantize_late_y(j, 1)
+            store_words(j)
+        store_late_scales([nc.scalar, nc.sync])

@@ -23,7 +23,7 @@ TILES = TOKENS // P
 GC = C // K_PASS
 GF = F // K_PASS
 RING_BANKS = 6
-EARLY_TILES = TILES - 3
+POOL_COLS = 256
 
 
 def tile_scaled_mixer_channel_mixing_h1_kernel(
@@ -61,13 +61,12 @@ def tile_scaled_mixer_channel_mixing_h1_kernel(
         os_rows = keep.tile([P, C // P], BF16, name="os_rows")
         b2_rows = keep.tile([P, C // P], BF16, name="b2_rows")
         hs_banks = [psum.tile([P, BANK], F32, name="hs_bank%d" % h) for h in range(2)]
-        hs_first = keep.tile([P, BANK], BF16, name="hs_first", align_bytes=64)
+        hs_first = keep.tile([P, POOL_COLS], BF16, name="hs_first", align_bytes=64)
         os_all = keep.tile([P, C], BF16, name="os_all", align_bytes=64)
         b2_all = keep.tile([P, C], BF16, name="b2_all", align_bytes=64)
         osb_all = keep.tile([P, C], F32, name="osb_all", align_bytes=64)
-        y_codes = keep.tile([P, TILES, GC, P], U32, name="y_codes", align_bytes=64)
-        y_scales = keep.tile([P, EARLY_TILES, GC, P], U8, name="y_scales", align_bytes=64)
-        late_scales = keep.tile([P, GC, TILES - EARLY_TILES, P], U8, name="late_scales", align_bytes=64)
+        y_codes = keep.tile([P, GC, TOKENS], U32, name="y_codes", align_bytes=64)
+        y_scales = keep.tile([P, GC, TOKENS], U8, name="y_scales", align_bytes=64)
         warm = keep.tile([P, 1], F32, name="warm")
 
         def load_rows(dst, rows, j):
@@ -204,11 +203,11 @@ def tile_scaled_mixer_channel_mixing_h1_kernel(
 
         def scale_first_chunk(j):
             nc.gpsimd.tensor_tensor(
-                out=hidden_tile(j, 0)[:, 0:BANK], in0=st["act", j, 0][:, 0:BANK], in1=hs_first[:], op=ALU.mult
+                out=hidden_tile(j, 0)[:, 0:POOL_COLS], in0=st["act", j, 0][:, 0:POOL_COLS], in1=hs_first[:], op=ALU.mult
             )
 
         def keep_first_chunk():
-            nc.vector.tensor_copy(out=hs_first[:].bitcast(F32), in_=hs_banks[0][:, 0 : BANK // 2])
+            nc.vector.tensor_copy(out=hs_first[:].bitcast(F32), in_=hs_banks[0][:, 0 : POOL_COLS // 2])
 
         def turn_h(j, h):
             words = st["hid", j, h][:].bitcast(F32)
@@ -220,11 +219,11 @@ def tile_scaled_mixer_channel_mixing_h1_kernel(
                 mx_pass(bank, ("h", j), g, w2, w2s, n, g == 0, g == GF - 1)
             st["o", j, n] = bank
 
-        def residual(j, n):
+        def residual(j, lo, hi):
             if ("res", j) not in st:
                 res = deep.tile([P, C], F32, name="res", tag="res", align_bytes=64)
                 st["res", j] = res
-            cols = slice(n * BANK, (n + 1) * BANK)
+            cols = slice(lo, hi)
             nc.gpsimd.tensor_tensor(out=st["res", j][:, cols], in0=skips[j][:, cols], in1=osb_all[:, cols], op=ALU.add)
 
         def scale_out(j, n):
@@ -256,37 +255,25 @@ def tile_scaled_mixer_channel_mixing_h1_kernel(
             words = st["y16", j][:].bitcast(F32)
             turn(("y", j), [words[:, (GC * u + g) * P : (GC * u + g + 1) * P] for g in range(GC) for u in range(2)])
 
-        def store_words(j):
+        def quantize_y(j, g):
+            nc.vector.quantize_mx(
+                out=y_codes[:, g, j * P : (j + 1) * P].bitcast(FP8X4),
+                scales=y_scales[:, g, j * P : (j + 1) * P],
+                in_=st[("y", j), "grouped"][:, g * K_PASS : (g + 1) * K_PASS],
+            )
+
+        def store_words(first, end):
             nc.sync.dma_start(
-                out=words_out[:, :, 4 * P * j : 4 * P * (j + 1)].bitcast(I32), in_=y_codes[:, j, :, :].bitcast(I32)
+                out=words_out[:, :, 4 * P * first : 4 * P * end].bitcast(I32),
+                in_=y_codes[:, :, first * P : end * P].bitcast(I32),
             )
 
-        def quantize_y(j):
-            nc.vector.quantize_mx(
-                out=y_codes[:, j, :, :].rearrange("p g m -> p (g m)").bitcast(FP8X4),
-                scales=y_scales[:, j, :, :].rearrange("p g m -> p (g m)"),
-                in_=st[("y", j), "grouped"][:, 0:C],
-            )
-            store_words(j)
-
-        def quantize_late(j, g, grouped):
-            nc.vector.quantize_mx(
-                out=y_codes[:, j, g, :].bitcast(FP8X4), scales=late_scales[:, g, j - EARLY_TILES, :], in_=grouped
-            )
-
-        def store_early_scales():
-            for q in range(4):
-                for g in range(GC):
-                    nc.sync.dma_start(
-                        out=out_2[g, 4 * q : 4 * q + 4, 0 : EARLY_TILES * P].rearrange("r (j m) -> r j m", m=P).bitcast(I32),
-                        in_=y_scales[32 * q : 32 * q + 4, :, g, :].bitcast(I32),
-                    )
-
-        def store_late_scales(queues):
+        def store_scales(first, end, queues):
+            cols = slice(first * P, end * P)
             for q in range(4):
                 queues[q % len(queues)].dma_start(
-                    out=out_2[:, 4 * q : 4 * q + 4, EARLY_TILES * P : TOKENS].rearrange("g r m -> r g m").bitcast(I32),
-                    in_=late_scales[32 * q : 32 * q + 4, :, :, :].rearrange("r g j m -> r g (j m)").bitcast(I32),
+                    out=out_2[:, 4 * q : 4 * q + 4, cols].rearrange("g r m -> r g m").bitcast(I32),
+                    in_=y_scales[32 * q : 32 * q + 4, :, cols].bitcast(I32),
                 )
 
         def round_last(j, g, direct):
@@ -324,9 +311,6 @@ def tile_scaled_mixer_channel_mixing_h1_kernel(
             words = st["y16_last", g][:].bitcast(F32)
             turn_half(("y", TILES - 1), g, [words[:, u * P : (u + 1) * P] for u in range(2)])
 
-        def quantize_late_y(j, g):
-            quantize_late(j, g, st[("y", j), "grouped"][:, g * K_PASS : (g + 1) * K_PASS])
-
         def live(j):
             return 0 <= j < TILES
 
@@ -357,12 +341,12 @@ def tile_scaled_mixer_channel_mixing_h1_kernel(
         for c in range(GF):
             stage1(1, c)
             gelu(1, c)
-        residual(0, 0)
-        residual(0, 1)
+        residual(0, 0, BANK)
+        residual(0, BANK, C)
         scale_first_chunk(1)
-        residual(1, 0)
-        residual(1, 1)
-        scale_hidden(1, 0, BANK)
+        residual(1, 0, BANK)
+        residual(1, BANK, C)
+        scale_hidden(1, 0, POOL_COLS)
         scale_hidden(1, 1)
 
         last = TILES - 1
@@ -378,7 +362,10 @@ def tile_scaled_mixer_channel_mixing_h1_kernel(
             if live(i - 4):
                 gather(("y", i - 4))
             if live(i - 5):
-                quantize_y(i - 5)
+                quantize_y(i - 5, 0)
+                quantize_y(i - 5, 1)
+            if i - 5 == 1:
+                store_words(0, 2)
             quantize(("h", i - 2), [0, 1, 2, 3])
             quantize(("x", i + 1), [0, 1])
             if live(i - 3):
@@ -387,14 +374,13 @@ def tile_scaled_mixer_channel_mixing_h1_kernel(
             for c in range(GF):
                 stage1(i, c)
                 gelu(i, c)
-            residual(i, 0)
-            residual(i, 1)
+            residual(i, 0, C)
             scale_first_chunk(i)
             if live(i - 3):
                 round_y(i - 3)
             stage2(i - 2, 0)
             stage2(i - 2, 1)
-            scale_hidden(i, 0, BANK)
+            scale_hidden(i, 0, POOL_COLS)
             scale_hidden(i, 1)
             scale_out(i - 2, 0)
             scale_out(i - 2, 1)
@@ -404,15 +390,15 @@ def tile_scaled_mixer_channel_mixing_h1_kernel(
         turn_h(a, 1)
         gather(("h", a), 0)
         gather(("h", a), 1)
-        quantize_y(a - 3)
+        quantize_y(a - 3, 0)
+        quantize_y(a - 3, 1)
         quantize(("h", a), [0, 1, 2, 3])
         add_out(a - 1, 0, C)
         store_y(a - 1, 0, C)
         for c in range(GF):
             stage1(z, c)
             gelu(z, c)
-        residual(z, 0)
-        residual(z, 1)
+        residual(z, 0, C)
         scale_hidden(z, 0)
         stage2(a, 0)
         turn_h(b, 0)
@@ -430,20 +416,23 @@ def tile_scaled_mixer_channel_mixing_h1_kernel(
         quantize(("h", b), [0, 1, 2, 3])
         scale_out(a, 1)
         gather(("y", a - 2))
-        gather(("y", a - 1))
         gather(("h", z), 0)
         gather(("h", z), 1)
-        quantize_y(a - 2)
+        gather(("y", a - 1))
+        quantize_y(a - 2, 0)
+        quantize_y(a - 2, 1)
+        store_words(a - 3, a - 1)
         add_out(a, 0, C)
         store_y(a, 0, C)
         round_y(a)
         stage2(b, 0)
         stage2(b, 1)
-        quantize_y(a - 1)
-        store_early_scales()
-        quantize(("h", z), [0, 1])
+        quantize(("h", z), [0, 1, 2, 3])
         scale_out(b, 0)
-        quantize(("h", z), [2, 3])
+        quantize_y(a - 1, 0)
+        quantize_y(a - 1, 1)
+        store_words(a - 1, a)
+        store_scales(0, a, [nc.sync])
         scale_out(b, 1)
         stage2(z, 0)
         stage2(z, 1)
@@ -466,7 +455,7 @@ def tile_scaled_mixer_channel_mixing_h1_kernel(
         turn_last(0)
         turn_last(1)
         for j in (a, b, z):
-            quantize_late_y(j, 0)
-            quantize_late_y(j, 1)
-            store_words(j)
-        store_late_scales([nc.scalar, nc.sync])
+            quantize_y(j, 0)
+            quantize_y(j, 1)
+            store_words(j, j + 1)
+        store_scales(a, TILES, [nc.scalar, nc.sync])

@@ -119,7 +119,7 @@ def tile_scaled_mixer_channel_mixing_h1_kernel(
         def spread_channels(rows, dst):
             bank = next_bank()
             spread(bank, rows[:].bitcast(F32))
-            nc.scalar.copy(
+            nc.vector.tensor_copy(
                 out=dst[:].bitcast(F32).rearrange("p (n w) -> p n w", w=4),
                 in_=bank[:].rearrange("p (w n) -> p n w", w=4),
             )
@@ -201,9 +201,9 @@ def tile_scaled_mixer_channel_mixing_h1_kernel(
                 out=hidden_tile(j, h)[:, lo:], in0=st["act", j, h][:, lo:], in1=hs_banks[h][:].bitcast(BF16)[:, lo:], op=ALU.mult
             )
 
-        def scale_first_chunk(j):
+        def scale_first_chunk(j, cols=POOL_COLS):
             nc.gpsimd.tensor_tensor(
-                out=hidden_tile(j, 0)[:, 0:POOL_COLS], in0=st["act", j, 0][:, 0:POOL_COLS], in1=hs_first[:], op=ALU.mult
+                out=hidden_tile(j, 0)[:, 0:cols], in0=st["act", j, 0][:, 0:cols], in1=hs_first[:, 0:cols], op=ALU.mult
             )
 
         def keep_first_chunk():
@@ -218,6 +218,10 @@ def tile_scaled_mixer_channel_mixing_h1_kernel(
             for g in range(GF):
                 mx_pass(bank, ("h", j), g, w2, w2s, n, g == 0, g == GF - 1)
             st["o", j, n] = bank
+
+        def scaled_bias(n):
+            cols = slice(n * BANK, (n + 1) * BANK)
+            nc.vector.tensor_tensor(out=osb_all[:, cols], in0=os_all[:, cols], in1=b2_all[:, cols], op=ALU.mult)
 
         def residual(j, lo, hi):
             if ("res", j) not in st:
@@ -262,10 +266,10 @@ def tile_scaled_mixer_channel_mixing_h1_kernel(
                 in_=st[("y", j), "grouped"][:, g * K_PASS : (g + 1) * K_PASS],
             )
 
-        def store_words(first, end):
-            nc.sync.dma_start(
-                out=words_out[:, :, 4 * P * first : 4 * P * end].bitcast(I32),
-                in_=y_codes[:, :, first * P : end * P].bitcast(I32),
+        def store_words(first, end, groups=slice(0, GC), queue=nc.sync):
+            queue.dma_start(
+                out=words_out[:, groups, 4 * P * first : 4 * P * end].bitcast(I32),
+                in_=y_codes[:, groups, first * P : end * P].bitcast(I32),
             )
 
         def store_scales(first, end, queues):
@@ -320,15 +324,17 @@ def tile_scaled_mixer_channel_mixing_h1_kernel(
         quantize(("x", 0), [0])
         quantize(("x", 0), [1])
         spread_channels(b2_rows, b2_all)
-        nc.vector.tensor_tensor(out=osb_all[:], in0=os_all[:], in1=b2_all[:], op=ALU.mult)
+        scaled_bias(0)
         for c in range(2):
             stage1(0, c)
             gelu(0, c)
         turn_x(1)
         spread_hidden(0)
         gather(("x", 1), copy=nc.vector.tensor_copy)
-        keep_first_chunk()
         quantize(("x", 1), [0, 1])
+        scaled_bias(1)
+        residual(0, BANK, C)
+        residual(0, 0, BANK)
         for c in range(2, GF):
             stage1(0, c)
             gelu(0, c)
@@ -338,14 +344,12 @@ def tile_scaled_mixer_channel_mixing_h1_kernel(
         gather(("x", 2), copy=nc.vector.tensor_copy)
         scale_hidden(0, 1)
         quantize(("x", 2), [0, 1])
+        keep_first_chunk()
         for c in range(GF):
             stage1(1, c)
             gelu(1, c)
-        residual(0, 0, BANK)
-        residual(0, BANK, C)
         scale_first_chunk(1)
         residual(1, 0, BANK)
-        residual(1, BANK, C)
         scale_hidden(1, 0, POOL_COLS)
         scale_hidden(1, 1)
 
@@ -374,8 +378,13 @@ def tile_scaled_mixer_channel_mixing_h1_kernel(
             for c in range(GF):
                 stage1(i, c)
                 gelu(i, c)
-            residual(i, 0, C)
-            scale_first_chunk(i)
+            if i == 2:
+                scale_first_chunk(2)
+                residual(1, BANK, C)
+                residual(2, 0, C)
+            else:
+                residual(i, 0, C)
+                scale_first_chunk(i)
             if live(i - 3):
                 round_y(i - 3)
             stage2(i - 2, 0)
@@ -400,22 +409,22 @@ def tile_scaled_mixer_channel_mixing_h1_kernel(
             gelu(z, c)
         residual(z, 0, C)
         scale_hidden(z, 0)
-        stage2(a, 0)
         turn_h(b, 0)
         turn_h(b, 1)
-        round_y(a - 1)
+        turn_y(a - 2)
         gather(("h", b), 0)
         gather(("h", b), 1)
-        scale_out(a, 0)
-        scale_hidden(z, 1)
+        gather(("y", a - 2))
+        round_y(a - 1)
+        stage2(a, 0)
         stage2(a, 1)
-        turn_y(a - 2)
-        turn_y(a - 1)
+        scale_hidden(z, 1)
+        scale_out(a, 0)
         turn_h(z, 0)
         turn_h(z, 1)
+        turn_y(a - 1)
         quantize(("h", b), [0, 1, 2, 3])
         scale_out(a, 1)
-        gather(("y", a - 2))
         gather(("h", z), 0)
         gather(("h", z), 1)
         gather(("y", a - 1))
@@ -448,14 +457,20 @@ def tile_scaled_mixer_channel_mixing_h1_kernel(
         gather(("y", a))
         round_last(z, 0, False)
         round_last(z, 1, True)
+        quantize_y(a, 0)
+        quantize_y(a, 1)
+        store_words(a, b)
         add_out(z, BANK, C)
         store_y(z, BANK, C)
         turn_y(b)
         gather(("y", b))
         turn_last(0)
         turn_last(1)
-        for j in (a, b, z):
-            quantize_y(j, 0)
-            quantize_y(j, 1)
-            store_words(j, j + 1)
-        store_scales(a, TILES, [nc.scalar, nc.sync])
+        quantize_y(b, 0)
+        quantize_y(b, 1)
+        store_words(b, z)
+        quantize_y(z, 0)
+        store_words(z, TILES, slice(0, 1))
+        quantize_y(z, 1)
+        store_words(z, TILES, slice(1, 2), nc.scalar)
+        store_scales(a, TILES, [nc.sync, nc.scalar])

from contextlib import ExitStack

import concourse.mybir as mybir
from concourse.masks import make_identity

TOKENS, C, F = 1024, 1024, 2048
FLOPS = 2 * 2 * TOKENS * C * F

F32 = mybir.dt.float32
BF16 = mybir.dt.bfloat16
I32 = mybir.dt.int32
U32 = mybir.dt.uint32
U8 = mybir.dt.uint8
FP8X4 = mybir.dt.float8_e4m3fn_x4
FP4X4 = mybir.dt.float4_e2m1fn_x4
ACT = mybir.ActivationFunctionType
ALU = mybir.AluOpType

P = 128
BANK = 512
K_PASS = 512
TILES = TOKENS // P
GC = C // K_PASS
GF = F // K_PASS
RING_BANKS = 6
POOL_COLS = 256


def tile_scaled_mixer_channel_mixing_h1_kernel(
    tc, x, w1_words, w1_scales, hid_scale, w2_words, w2_scales, b2, out_scale, skip, out_0, out_1, out_2
):
    nc = tc.nc
    x_rows = x.rearrange("b p c -> (b p) c")
    skip_rows = skip.rearrange("b p c -> (b p) c")
    y_rows = out_0.rearrange("b p c -> (b p) c")
    words_out = out_1.rearrange("g p m t -> p g (m t)")

    with ExitStack() as ctx:
        keep = ctx.enter_context(tc.tile_pool(name="keep", bufs=1))
        work = ctx.enter_context(tc.tile_pool(name="work", bufs=2))
        deep = ctx.enter_context(tc.tile_pool(name="deep", bufs=3))
        psum = ctx.enter_context(tc.psum_pool(name="psum", bufs=1))
        ctx.enter_context(tc.manual_schedule())

        taken = []

        def next_bank():
            tag = "bank%d" % (len(taken) % RING_BANKS)
            bank = psum.tile([P, BANK], F32, name=tag, tag=tag)
            taken.append(bank)
            return bank

        ident = keep.tile([P, P], F32, name="ident")
        w1 = [keep.tile([P, GC, 2 * BANK], U8, name="w1_%d" % c, align_bytes=64) for c in range(GF)]
        w2 = [keep.tile([P, GF, 2 * BANK], U8, name="w2_%d" % n, align_bytes=64) for n in range(GC)]
        w1s = keep.tile([P, GC, F], U8, name="w1s", align_bytes=64)
        w2s = keep.tile([P, GF, C], U8, name="w2s", align_bytes=64)
        xs = [keep.tile([P, C], BF16, name="x_%d" % j, align_bytes=64) for j in range(TILES)]
        skips = [keep.tile([P, C], BF16, name="skip_%d" % j, align_bytes=64) for j in range(TILES)]
        hs_rows = keep.tile([P, GF, 4], BF16, name="hs_rows")
        os_rows = keep.tile([P, C // P], BF16, name="os_rows")
        b2_rows = keep.tile([P, C // P], BF16, name="b2_rows")
        hs_banks = [psum.tile([P, BANK], F32, name="hs_bank%d" % h) for h in range(2)]
        hs_first = keep.tile([P, POOL_COLS], BF16, name="hs_first", align_bytes=64)
        os_all = keep.tile([P, C], BF16, name="os_all", align_bytes=64)
        b2_all = keep.tile([P, C], BF16, name="b2_all", align_bytes=64)
        osb_all = keep.tile([P, C], F32, name="osb_all", align_bytes=64)
        y_codes = keep.tile([P, GC, TOKENS], U32, name="y_codes", align_bytes=64)
        y_scales = keep.tile([P, GC, TOKENS], U8, name="y_scales", align_bytes=64)
        warm = keep.tile([P, 1], F32, name="warm")

        def load_rows(dst, rows, j):
            nc.sync.dma_start(out=dst[j][:], in_=rows[j * P : (j + 1) * P, :])

        def load_words(dst, words, c):
            src = words.rearrange("g p n -> p g n")[:, :, 2 * BANK * c : 2 * BANK * (c + 1)]
            nc.sync.dma_start(out=dst[c][:].bitcast(I32), in_=src.bitcast(I32))

        def load_scales(dst, scales, lo, hi):
            for q in range(4):
                src = scales[:, 4 * q : 4 * q + 4, lo:hi].rearrange("g r n -> r g n")
                nc.sync.dma_start(out=dst[32 * q : 32 * q + 4, :, lo:hi].bitcast(I32), in_=src.bitcast(I32))

        nc.scalar.dma_start(out=os_rows[:], in_=out_scale.rearrange("(p k) -> p k", p=P))
        nc.scalar.dma_start(out=b2_rows[:], in_=b2.rearrange("(p k) -> p k", p=P))
        nc.vector.memset(w1s[:].bitcast(I32), 0)
        nc.vector.memset(w2s[:].bitcast(I32), 0)
        make_identity(nc, ident[:])
        nc.scalar.activation(out=warm[:], in_=ident[:, 0:1], func=ACT.Gelu_apprx_tanh)

        load_rows(xs, x_rows, 0)
        load_scales(w1s, w1_scales, 0, F // 2)
        load_words(w1, w1_words, 0)
        nc.sync.dma_start(out=hs_rows[:], in_=hid_scale.rearrange("(g p k) -> p g k", g=GF, p=P))
        load_words(w1, w1_words, 1)
        load_rows(xs, x_rows, 1)
        load_scales(w1s, w1_scales, F // 2, F)
        load_words(w1, w1_words, 2)
        load_words(w1, w1_words, 3)
        load_rows(xs, x_rows, 2)
        load_rows(skips, skip_rows, 0)
        load_rows(skips, skip_rows, 1)
        load_scales(w2s, w2_scales, 0, C)
        load_rows(xs, x_rows, 3)
        load_words(w2, w2_words, 0)
        load_rows(skips, skip_rows, 2)
        load_words(w2, w2_words, 1)
        for j in range(4, TILES):
            load_rows(xs, x_rows, j)
            load_rows(skips, skip_rows, j - 1)
        load_rows(skips, skip_rows, TILES - 1)

        st = {}

        def spread(bank, words):
            for s in range(4):
                nc.tensor.transpose(bank[:, s * P : (s + 1) * P], words[:, s : s + 1].to_broadcast([P, P]), ident[:])

        def spread_channels(rows, dst):
            bank = next_bank()
            spread(bank, rows[:].bitcast(F32))
            nc.vector.tensor_copy(
                out=dst[:].bitcast(F32).rearrange("p (n w) -> p n w", w=4),
                in_=bank[:].rearrange("p (w n) -> p n w", w=4),
            )

        def spread_hidden(h):
            words = hs_rows[:].rearrange("p g k -> p (g k)").bitcast(F32)
            spread(hs_banks[h], words[:, 4 * h : 4 * h + 4])

        def turn(key, sources, part=0):
            bank = next_bank()
            for s, src in enumerate(sources):
                nc.tensor.transpose(bank[:, s * P : (s + 1) * P], src, ident[:])
            st[key, "bank", part] = bank

        def gather(key, part=0, copy=nc.scalar.copy):
            if part == 0:
                grouped = deep.tile([P, F], BF16, name="grouped", tag="grouped", align_bytes=64, bufs=5)
                st[key, "grouped"] = grouped
            dst = st[key, "grouped"][:, part * 2 * K_PASS : (part + 1) * 2 * K_PASS]
            copy(
                out=dst.bitcast(F32).rearrange("p (g r u) -> p g r u", g=2, u=2),
                in_=st[key, "bank", part][:].rearrange("p (g u r) -> p g r u", g=2, u=2),
            )

        def quantize(key, groups):
            if groups[0] == 0:
                codes = deep.tile([P, GF * P], U32, name="codes", tag="codes", align_bytes=64, bufs=4)
                scales = deep.tile([P, GF * P], U8, name="scales", tag="scales", align_bytes=64, bufs=4)
                st[key, "mx"] = (codes, scales)
            codes, scales = st[key, "mx"]
            lo, hi = groups[0], groups[-1] + 1
            nc.vector.quantize_mx(
                out=codes[:, lo * P : hi * P].bitcast(FP8X4),
                scales=scales[:, lo * P : hi * P],
                in_=st[key, "grouped"][:, lo * K_PASS : hi * K_PASS],
            )

        def mx_pass(bank, key, g, w, ws, c, start, stop):
            codes, scales = st[key, "mx"]
            nc.tensor.matmul_mx(
                out=bank[:],
                lhsT=codes[:, g * P : (g + 1) * P].bitcast(FP8X4),
                lhsT_scale=scales[:, g * P : (g + 1) * P],
                rhs=w[c][:, g, :].bitcast(FP4X4),
                rhs_scale=ws[:, g, c * BANK : (c + 1) * BANK],
                start=start,
                stop=stop,
            )

        def turn_x(j):
            words = xs[j][:].bitcast(F32)
            turn(("x", j), [words[:, 256 * g + u : 256 * (g + 1) : 2] for g in range(GC) for u in range(2)])

        def stage1(j, c):
            bank = next_bank()
            for g in range(GC):
                mx_pass(bank, ("x", j), g, w1, w1s, c, g == 0, g == GC - 1)
            st["z", j, c] = bank

        def gelu(j, c):
            if c % 2 == 0:
                act = deep.tile([P, 2 * BANK], F32, name="act", tag="act", align_bytes=64, bufs=4)
                st["act", j, c // 2] = act
            act = st["act", j, c // 2]
            nc.scalar.activation(
                out=act[:, (c % 2) * BANK : (c % 2 + 1) * BANK].rearrange("p (u q e) -> p u q e", u=2, e=2),
                in_=st["z", j, c][:].rearrange("p (q u e) -> p u q e", u=2, e=2),
                func=ACT.Gelu_apprx_tanh,
            )

        def hidden_tile(j, h):
            if ("hid", j, h) not in st:
                hid = deep.tile([P, 2 * BANK], BF16, name="hid", tag="hid", align_bytes=64, bufs=4)
                st["hid", j, h] = hid
            return st["hid", j, h]

        def scale_hidden(j, h, lo=0):
            nc.vector.tensor_tensor(
                out=hidden_tile(j, h)[:, lo:], in0=st["act", j, h][:, lo:], in1=hs_banks[h][:].bitcast(BF16)[:, lo:], op=ALU.mult
            )

        def scale_first_chunk(j, cols=POOL_COLS):
            nc.gpsimd.tensor_tensor(
                out=hidden_tile(j, 0)[:, 0:cols], in0=st["act", j, 0][:, 0:cols], in1=hs_first[:, 0:cols], op=ALU.mult
            )

        def keep_first_chunk():
            nc.vector.tensor_copy(out=hs_first[:].bitcast(F32), in_=hs_banks[0][:, 0 : POOL_COLS // 2])

        def turn_h(j, h):
            words = st["hid", j, h][:].bitcast(F32)
            turn(("h", j), [words[:, s * P : (s + 1) * P] for s in range(4)], h)

        def stage2(j, n):
            bank = next_bank()
            for g in range(GF):
                mx_pass(bank, ("h", j), g, w2, w2s, n, g == 0, g == GF - 1)
            st["o", j, n] = bank

        def scaled_bias(n):
            cols = slice(n * BANK, (n + 1) * BANK)
            nc.vector.tensor_tensor(out=osb_all[:, cols], in0=os_all[:, cols], in1=b2_all[:, cols], op=ALU.mult)

        def residual(j, lo, hi):
            if ("res", j) not in st:
                res = deep.tile([P, C], F32, name="res", tag="res", align_bytes=64)
                st["res", j] = res
            cols = slice(lo, hi)
            nc.gpsimd.tensor_tensor(out=st["res", j][:, cols], in0=skips[j][:, cols], in1=osb_all[:, cols], op=ALU.add)

        def scale_out(j, n):
            if n == 0:
                branch = work.tile([P, C], F32, name="branch", tag="branch", align_bytes=64)
                st["branch", j] = branch
            cols = slice(n * BANK, (n + 1) * BANK)
            nc.vector.tensor_tensor(out=st["branch", j][:, cols], in0=st["o", j, n][:], in1=os_all[:, cols], op=ALU.mult)

        def add_out(j, lo, hi, engine=nc.vector):
            if ("y", j) not in st:
                y = deep.tile([P, C], F32, name="y", tag="y", align_bytes=64)
                st["y", j] = y
            y = st["y", j]
            engine.tensor_tensor(out=y[:, lo:hi], in0=st["branch", j][:, lo:hi], in1=st["res", j][:, lo:hi], op=ALU.add)

        def store_y(j, lo, hi):
            nc.sync.dma_start(out=y_rows[j * P : (j + 1) * P, lo:hi], in_=st["y", j][:, lo:hi])

        def round_y(j):
            y16 = work.tile([P, C], BF16, name="y16", tag="y16", align_bytes=64)
            nc.scalar.copy(
                out=y16[:].rearrange("p (u q e) -> p u q e", u=2, e=2),
                in_=st["y", j][:].rearrange("p (q u e) -> p u q e", u=2, e=2),
            )
            st["y16", j] = y16

        def turn_y(j):
            words = st["y16", j][:].bitcast(F32)
            turn(("y", j), [words[:, (GC * u + g) * P : (GC * u + g + 1) * P] for g in range(GC) for u in range(2)])

        def quantize_y(j, g):
            nc.vector.quantize_mx(
                out=y_codes[:, g, j * P : (j + 1) * P].bitcast(FP8X4),
                scales=y_scales[:, g, j * P : (j + 1) * P],
                in_=st[("y", j), "grouped"][:, g * K_PASS : (g + 1) * K_PASS],
            )

        def store_words(first, end, groups=slice(0, GC), queue=nc.sync):
            queue.dma_start(
                out=words_out[:, groups, 4 * P * first : 4 * P * end].bitcast(I32),
                in_=y_codes[:, groups, first * P : end * P].bitcast(I32),
            )

        def store_scales(first, end, queues):
            cols = slice(first * P, end * P)
            for q in range(4):
                queues[q % len(queues)].dma_start(
                    out=out_2[:, 4 * q : 4 * q + 4, cols].rearrange("g r m -> r g m").bitcast(I32),
                    in_=y_scales[32 * q : 32 * q + 4, :, cols].bitcast(I32),
                )

        def round_last(j, g, direct):
            cols = slice(g * BANK, (g + 1) * BANK)
            y16 = work.tile([P, BANK], BF16, name="y16_last", tag="y16_last", align_bytes=64)
            word_order = y16[:].rearrange("p (u q e) -> p u q e", u=2, e=2)
            if direct:
                nc.vector.tensor_tensor(
                    out=word_order,
                    in0=st["branch", j][:, cols].rearrange("p (q u e) -> p u q e", u=2, e=2),
                    in1=st["res", j][:, cols].rearrange("p (q u e) -> p u q e", u=2, e=2),
                    op=ALU.add,
                )
            else:
                nc.scalar.copy(out=word_order, in_=st["y", j][:, cols].rearrange("p (q u e) -> p u q e", u=2, e=2))
            st["y16_last", g] = y16

        def turn_half(key, g, sources):
            bank = next_bank()
            for u, src in enumerate(sources):
                nc.tensor.transpose(bank[:, u * P : (u + 1) * P], src, ident[:])
            if g == 0:
                grouped = deep.tile([P, F], BF16, name="grouped", tag="grouped", align_bytes=64, bufs=5)
                st[key, "grouped"] = grouped
            nc.scalar.copy(
                out=st[key, "grouped"][:, g * K_PASS : (g + 1) * K_PASS].bitcast(F32).rearrange("p (r u) -> p r u", u=2),
                in_=bank[:, 0 : 2 * P].rearrange("p (u r) -> p r u", u=2),
            )

        def turn_first(g):
            words = xs[0][:].bitcast(F32)
            turn_half(("x", 0), g, [words[:, 256 * g + u : 256 * (g + 1) : 2] for u in range(2)])

        def turn_last(g):
            words = st["y16_last", g][:].bitcast(F32)
            turn_half(("y", TILES - 1), g, [words[:, u * P : (u + 1) * P] for u in range(2)])

        def live(j):
            return 0 <= j < TILES

        spread_channels(os_rows, os_all)
        turn_first(0)
        turn_first(1)
        quantize(("x", 0), [0])
        quantize(("x", 0), [1])
        spread_channels(b2_rows, b2_all)
        scaled_bias(0)
        for c in range(2):
            stage1(0, c)
            gelu(0, c)
        turn_x(1)
        spread_hidden(0)
        gather(("x", 1), copy=nc.vector.tensor_copy)
        quantize(("x", 1), [0, 1])
        scaled_bias(1)
        residual(0, BANK, C)
        residual(0, 0, BANK)
        for c in range(2, GF):
            stage1(0, c)
            gelu(0, c)
        scale_hidden(0, 0)
        turn_x(2)
        spread_hidden(1)
        gather(("x", 2), copy=nc.vector.tensor_copy)
        scale_hidden(0, 1)
        quantize(("x", 2), [0, 1])
        keep_first_chunk()
        for c in range(GF):
            stage1(1, c)
            gelu(1, c)
        scale_first_chunk(1)
        residual(1, 0, BANK)
        scale_hidden(1, 0, POOL_COLS)
        scale_hidden(1, 1)

        last = TILES - 1
        for i in range(2, last):
            turn_h(i - 2, 0)
            turn_h(i - 2, 1)
            turn_x(i + 1)
            if live(i - 4):
                turn_y(i - 4)
            gather(("h", i - 2), 0)
            gather(("h", i - 2), 1)
            gather(("x", i + 1))
            if live(i - 4):
                gather(("y", i - 4))
            if live(i - 5):
                quantize_y(i - 5, 0)
                quantize_y(i - 5, 1)
            if i - 5 == 1:
                store_words(0, 2)
            quantize(("h", i - 2), [0, 1, 2, 3])
            quantize(("x", i + 1), [0, 1])
            if live(i - 3):
                add_out(i - 3, 0, C)
                store_y(i - 3, 0, C)
            for c in range(GF):
                stage1(i, c)
                gelu(i, c)
            if i == 2:
                scale_first_chunk(2)
                residual(1, BANK, C)
                residual(2, 0, C)
            else:
                residual(i, 0, C)
                scale_first_chunk(i)
            if live(i - 3):
                round_y(i - 3)
            stage2(i - 2, 0)
            stage2(i - 2, 1)
            scale_hidden(i, 0, POOL_COLS)
            scale_hidden(i, 1)
            scale_out(i - 2, 0)
            scale_out(i - 2, 1)

        a, b, z = last - 2, last - 1, last
        turn_h(a, 0)
        turn_h(a, 1)
        gather(("h", a), 0)
        gather(("h", a), 1)
        quantize_y(a - 3, 0)
        quantize_y(a - 3, 1)
        quantize(("h", a), [0, 1, 2, 3])
        add_out(a - 1, 0, C)
        store_y(a - 1, 0, C)
        for c in range(GF):
            stage1(z, c)
            gelu(z, c)
        residual(z, 0, C)
        scale_hidden(z, 0)
        turn_h(b, 0)
        turn_h(b, 1)
        turn_y(a - 2)
        gather(("h", b), 0)
        gather(("h", b), 1)
        gather(("y", a - 2))
        round_y(a - 1)
        stage2(a, 0)
        stage2(a, 1)
        scale_hidden(z, 1)
        scale_out(a, 0)
        turn_h(z, 0)
        turn_h(z, 1)
        turn_y(a - 1)
        quantize(("h", b), [0, 1, 2, 3])
        scale_out(a, 1)
        gather(("h", z), 0)
        gather(("h", z), 1)
        gather(("y", a - 1))
        quantize_y(a - 2, 0)
        quantize_y(a - 2, 1)
        store_words(a - 3, a - 1)
        add_out(a, 0, C)
        store_y(a, 0, C)
        round_y(a)
        stage2(b, 0)
        stage2(b, 1)
        quantize(("h", z), [0, 1, 2, 3])
        scale_out(b, 0)
        quantize_y(a - 1, 0)
        quantize_y(a - 1, 1)
        store_words(a - 1, a)
        store_scales(0, a, [nc.sync])
        scale_out(b, 1)
        stage2(z, 0)
        stage2(z, 1)
        add_out(b, 0, BANK)
        add_out(b, BANK, C)
        store_y(b, 0, C)
        round_y(b)
        scale_out(z, 0)
        scale_out(z, 1)
        add_out(z, 0, BANK)
        store_y(z, 0, BANK)
        turn_y(a)
        gather(("y", a))
        round_last(z, 0, False)
        round_last(z, 1, True)
        quantize_y(a, 0)
        quantize_y(a, 1)
        store_words(a, b)
        add_out(z, BANK, C)
        store_y(z, BANK, C)
        turn_y(b)
        gather(("y", b))
        turn_last(0)
        turn_last(1)
        quantize_y(b, 0)
        quantize_y(b, 1)
        store_words(b, z)
        quantize_y(z, 0)
        store_words(z, TILES, slice(0, 1))
        quantize_y(z, 1)
        store_words(z, TILES, slice(1, 2), nc.scalar)
        store_scales(a, TILES, [nc.sync, nc.scalar])
